import numpy as np
import ml_dtypes


def mxq(x, axis, fmt="e4m3"):
    dtype, down = {"e4m3": (ml_dtypes.float8_e4m3fn, 7), "e5m2": (ml_dtypes.float8_e5m2, 14)}[fmt]
    v = np.moveaxis(np.asarray(x, np.float32).astype(ml_dtypes.bfloat16).astype(np.float64), axis, -1)
    blocks = v.reshape(v.shape[:-1] + (-1, 32))
    amax = np.abs(blocks).max(-1, keepdims=True)
    byte = np.maximum(np.where(amax > 0, np.frexp(amax)[1] - 1 + 127, 0) - down, 1)
    scale = np.exp2(byte - 127.0)
    codes = (blocks / scale).astype(np.float32).astype(dtype).astype(np.float64)
    return np.moveaxis((codes * scale).reshape(v.shape), -1, axis)


WIDE = False


def mx_kscale(k):
    if not WIDE:
        return np.ones(k)
    levels = np.array([10, -10, 5, -5, 0])
    if k % 512:
        return np.exp2(np.random.permutation(np.resize(levels, k // 32))).repeat(32)
    a = np.empty((k // 512, 16))
    for p in range(k // 512):
        a[p, :8] = np.random.permutation(np.resize(levels, 8))
        for g in range(8):
            far = levels[np.abs(levels - a[p, g]) >= 10]
            a[p, g + 8] = far[np.random.randint(len(far))]
    return np.exp2(a.ravel()).repeat(32)


BF16 = ml_dtypes.bfloat16


def bf(x):
    return np.asarray(x, np.float32).astype(BF16)


def f64(x):
    return np.asarray(x).astype(np.float64)


E2M1 = np.array([0.0, 0.5, 1.0, 1.5, 2.0, 3.0, 4.0, 6.0, -0.0, -0.5, -1.0, -1.5, -2.0, -3.0, -4.0, -6.0])


def pack_weight(w, fmt):
    k, n = w.shape
    w = f64(bf(w)).reshape(k // 32, 32, n)
    amax = np.abs(w).max(1)
    if fmt == "e4m3":
        byte = np.frexp(amax)[1] - 1 + 127 - 7
    else:
        mant, ex = np.frexp(amax / 6.0)
        byte = np.where(mant > 0.5, ex, ex - 1) + 127
    byte = np.clip(np.where(amax > 0, byte, 1), 1, 254)
    scaled = (w * np.exp2(127.0 - byte)[:, None, :]).reshape(k, n).astype(np.float32)
    by_word = np.ascontiguousarray(scaled.reshape(k // 512, 128, 4, n).transpose(0, 1, 3, 2))
    if fmt == "e4m3":
        words = by_word.astype(ml_dtypes.float8_e4m3fn).view(np.uint8)
    else:
        c = by_word.astype(ml_dtypes.float4_e2m1fn).view(np.uint8) & 0xF
        words = c[..., 0::2] | (c[..., 1::2] << 4)
    return np.ascontiguousarray(words), np.ascontiguousarray(byte.astype(np.uint8).reshape(k // 512, 16, n))


def unpack_weight(words, scales, fmt):
    g, p, n, _ = words.shape
    if fmt == "e4m3":
        vals = np.ascontiguousarray(words).view(ml_dtypes.float8_e4m3fn).astype(np.float64)
    else:
        nib = np.empty((g, p, n, 4), np.uint8)
        nib[..., 0::2] = words & 0xF
        nib[..., 1::2] = words >> 4
        vals = E2M1[nib]
    vals = vals * np.repeat(np.exp2(scales.astype(np.float64) - 127.0), 8, axis=1)[..., None]
    return vals.transpose(0, 1, 3, 2).reshape(g * 512, n)
def pack4(w):
    words, scales = pack_weight(w, "e2m1")
    return words.reshape(words.shape[0], 128, -1), scales


def unpack4(words, scales):
    return unpack_weight(words.reshape(words.shape[0], 128, -1, 2), scales, "e2m1")


M, K = 1024, 1024

SHARE = 0.33
SPREAD = 0.1


def setup_inputs():
    s, u, z = mx_kscale(K), mx_kscale(K), mx_kscale(K)
    x = bf(np.random.standard_normal((M, K)) * s)
    d1_words, d1_scales = pack4(SHARE * np.random.standard_normal((K, K)) / np.sqrt(K) / s[:, None] * s)
    d2_words, d2_scales = pack4(SHARE * np.random.standard_normal((K, K)) / np.sqrt(K) / u[:, None] * u)
    d3_words, d3_scales = pack4(SHARE * np.random.standard_normal((K, K)) / np.sqrt(K) / z[:, None] * z)
    return {"x": x,
            "d1_words": d1_words, "d1_scales": d1_scales,
            "d2_words": d2_words, "d2_scales": d2_scales,
            "d3_words": d3_words, "d3_scales": d3_scales,
            "v1": bf((1 + SPREAD * np.random.standard_normal(K)) * u / s),
            "v2": bf((1 + SPREAD * np.random.standard_normal(K)) * z / u),
            "v3": bf((1 + SPREAD * np.random.standard_normal(K)) / z)}


def reference(x, d1_words, d1_scales, d2_words, d2_scales, d3_words, d3_scales, v1, v2, v3):
    x = f64(x)
    c1 = mxq(x, 1, "e4m3") @ unpack4(d1_words, d1_scales)
    r1 = (x - c1) * f64(v1)
    c2 = mxq(r1, 1, "e4m3") @ unpack4(d2_words, d2_scales)
    r2 = (r1 - c2) * f64(v2)
    c3 = mxq(r2, 1, "e4m3") @ unpack4(d3_words, d3_scales)
    return (r2 - c3) * f64(v3)

@@ -1,0 +1,246 @@
+from contextlib import ExitStack
+
+import concourse.mybir as mybir
+from concourse.masks import make_identity
+
+F32 = mybir.dt.float32
+BF16 = mybir.dt.bfloat16
+I32 = mybir.dt.int32
+U32 = mybir.dt.uint32
+U8 = mybir.dt.uint8
+FP8X4 = mybir.dt.float8_e4m3fn_x4
+FP4X4 = mybir.dt.float4_e2m1fn_x4
+ALU = mybir.AluOpType
+COPY = mybir.ActivationFunctionType.Copy
+
+P = 128
+FRAMES = 1024
+MODES = 1024
+SLOTS = 4
+GROUP = P * SLOTS
+GROUPS = MODES // GROUP
+CHUNK = 512
+CHUNKS = FRAMES // CHUNK
+TILES = CHUNK // P
+STAGES = 3
+RUNS = STAGES * CHUNKS * GROUPS
+FLOPS = STAGES * 2 * FRAMES * MODES * MODES
+
+
+def tile_three_mirror_correction_t2_kernel(
+    tc, x, d1_words, d1_scales, d2_words, d2_scales, d3_words, d3_scales, v1, v2, v3, out
+):
+    nc = tc.nc
+    d_words = (d1_words, d2_words, d3_words)
+    d_scales = (d1_scales, d2_scales, d3_scales)
+    factors = (v1, v2, v3)
+
+    with ExitStack() as ctx:
+        keep = ctx.enter_context(tc.tile_pool(name="keep", bufs=1))
+        resid = ctx.enter_context(tc.tile_pool(name="resid", bufs=2))
+        stage_out = ctx.enter_context(tc.tile_pool(name="stage_out", bufs=8))
+        psum = ctx.enter_context(tc.psum_pool(name="psum", bufs=8))
+        ctx.enter_context(tc.manual_schedule())
+
+        def new(name, shape, dtype):
+            return keep.tile(shape, dtype, name=name, align_bytes=64)
+
+        ident = new("ident", [P, P], F32)
+        x_rows = [new("x_rows%d" % j, [P, MODES], BF16) for j in range(FRAMES // P)]
+        raw_codes = {(s, h): new("raw_codes%d%d" % (s, h), [P, GROUPS, 2 * GROUP], U8) for s in range(STAGES) for h in range(GROUPS)}
+        raw_scales = [new("raw_scales%d" % s, [P, GROUPS, MODES], U8) for s in range(STAGES)]
+        w_codes = {(s, h): new("w_codes%d%d" % (s, h), [P, GROUPS, SLOTS, 2 * P], U8) for s in range(STAGES) for h in range(GROUPS)}
+        w_scales = {(s, h): new("w_scales%d%d" % (s, h), [P, GROUPS, SLOTS, P], U8) for s in range(STAGES) for h in range(GROUPS)}
+        v_raw = [new("v_raw%d" % s, [P, GROUPS, SLOTS], BF16) for s in range(STAGES)]
+        v_neg = [new("v_neg%d" % s, [P, GROUPS, SLOTS], F32) for s in range(STAGES)]
+        v_run = [new("v_run%d" % q, [P, SLOTS], F32) for q in range(RUNS)]
+        x_packed = [new("x_packed%d" % c, [P, GROUPS, CHUNK * SLOTS], BF16) for c in range(CHUNKS)]
+        r_packed = [new("r_packed%d" % q, [P, CHUNK * SLOTS], BF16) for q in range(RUNS - CHUNKS * GROUPS)]
+        a_codes = {(s, c, g): new("a_codes%d%d%d" % (s, c, g), [P, CHUNK], U32) for s in range(STAGES) for c in range(CHUNKS) for g in range(GROUPS)}
+        a_scales = {(s, c, g): new("a_scales%d%d%d" % (s, c, g), [P, CHUNK], U8) for s in range(STAGES) for c in range(CHUNKS) for g in range(GROUPS)}
+        r_tiles = {}
+        banks = {}
+
+        def run_of(q):
+            return q // (CHUNKS * GROUPS), (q // GROUPS) % CHUNKS, q % GROUPS
+
+        def load_x(j):
+            nc.sync.dma_start(out=x_rows[j][:], in_=x[j * P : (j + 1) * P, :])
+
+        def load_factor(s):
+            nc.sync.dma_start(out=v_raw[s][:], in_=factors[s].rearrange("(g p t) -> p g t", p=P, t=SLOTS))
+
+        def load_codes(s, h):
+            src = d_words[s][:, :, 2 * GROUP * h : 2 * GROUP * (h + 1)].rearrange("g p n -> p g n")
+            nc.sync.dma_start(out=raw_codes[s, h][:].bitcast(I32), in_=src.bitcast(I32))
+
+        def load_scales(s):
+            for quad in range(4):
+                src = d_scales[s][:, 4 * quad : 4 * quad + 4, :].rearrange("g r n -> r g n")
+                nc.sync.dma_start(out=raw_scales[s][32 * quad : 32 * quad + 4, :, :].bitcast(I32), in_=src.bitcast(I32))
+
+        nc.vector.memset(raw_scales[0][:].bitcast(I32), 0)
+        make_identity(nc, ident[:])
+        nc.gpsimd.memset(raw_scales[1][:].bitcast(I32), 0)
+        nc.gpsimd.memset(raw_scales[2][:].bitcast(I32), 0)
+
+        load_x(0)
+        load_factor(0)
+        load_x(1)
+        load_codes(0, 0)
+        load_x(2)
+        load_x(3)
+        load_scales(0)
+        load_codes(0, 1)
+        for j in range(TILES, 2 * TILES):
+            load_x(j)
+        for s in (1, 2):
+            load_factor(s)
+            load_scales(s)
+            load_codes(s, 0)
+            load_codes(s, 1)
+
+        def negate(s):
+            nc.scalar.activation(out=v_neg[s][:], in_=v_raw[s][:], func=COPY, scale=-1.0)
+
+        def sort_weights(s, h):
+            nc.vector.tensor_copy(
+                out=w_codes[s, h][:].rearrange("p g t (m b) -> p g t m b", b=2),
+                in_=raw_codes[s, h][:].rearrange("p g (m t b) -> p g t m b", t=SLOTS, b=2),
+            )
+            nc.vector.tensor_copy(
+                out=w_scales[s, h][:],
+                in_=raw_scales[s][:, :, GROUP * h : GROUP * (h + 1)].rearrange("p g (m t) -> p g t m", t=SLOTS),
+            )
+
+        def turn_x(j):
+            bank = psum.tile([P, GROUPS, 2, P], F32, name="bank", tag="bank")
+            words = x_rows[j][:].bitcast(F32)
+            half = GROUP // 2
+            for g in range(GROUPS):
+                for u in range(2):
+                    nc.tensor.transpose(bank[:, g, u, :], words[:, half * g + u : half * (g + 1) : 2], ident[:])
+            banks["x", j] = bank
+
+        def pack_x(j):
+            c, jj = divmod(j, TILES)
+            dst = x_packed[c][:].bitcast(F32).rearrange("p g (r u) -> p g r u", u=2)
+            nc.scalar.copy(out=dst[:, :, jj * P : (jj + 1) * P, :], in_=banks["x", j][:].rearrange("p g u r -> p g r u"))
+
+        def quantize(s, c, g, src):
+            nc.vector.quantize_mx(out=a_codes[s, c, g][:].bitcast(FP8X4), scales=a_scales[s, c, g][:], in_=src)
+
+        def quantize_x(c):
+            for g in range(GROUPS):
+                quantize(0, c, g, x_packed[c][:, g, :])
+
+        def quantize_run(q):
+            s, c, h = run_of(q)
+            quantize(s + 1, c, h, r_packed[q][:])
+
+        def open_run(q, on_scalar):
+            s, c, h = run_of(q)
+            r_tiles[q] = resid.tile([P, SLOTS, CHUNK], F32, name="r%d%d" % (c, h), tag="r%d%d" % (c, h))
+            if on_scalar:
+                nc.scalar.copy(out=v_run[q][:], in_=v_raw[s][:, h, :])
+            else:
+                nc.vector.tensor_copy(out=v_run[q][:], in_=v_raw[s][:, h, :])
+
+        def carry(q, t, on_scalar):
+            s, c, h = run_of(q)
+            if s == 0:
+                src = x_packed[c][:, h, :].rearrange("p (n t) -> p t n", t=SLOTS)[:, t, :]
+            else:
+                src = r_tiles[q - CHUNKS * GROUPS][:, t, :]
+            dst = r_tiles[q][:, t, :]
+            factor = v_run[q][:, t : t + 1]
+            if on_scalar:
+                nc.scalar.activation(out=dst, in_=src, func=COPY, scale=factor)
+            else:
+                nc.gpsimd.tensor_scalar(out=dst, in0=src, scalar1=factor, scalar2=0.0, op0=ALU.mult, op1=ALU.add)
+
+        def step(q, t):
+            s, c, h = run_of(q)
+            bank = psum.tile([P, CHUNK], F32, name="bank", tag="bank")
+            for g in range(GROUPS):
+                nc.tensor.matmul_mx(
+                    out=bank[:],
+                    lhsT=w_codes[s, h][:, g, t, :].bitcast(FP4X4),
+                    lhsT_scale=w_scales[s, h][:, g, t, :],
+                    rhs=a_codes[s, c, g][:].bitcast(FP8X4),
+                    rhs_scale=a_scales[s, c, g][:],
+                    start=(g == 0),
+                    stop=(g == GROUPS - 1),
+                )
+            r = r_tiles[q][:, t, :]
+            nc.vector.scalar_tensor_tensor(
+                out=r, in0=bank[:], scalar=v_neg[s][:, h, t : t + 1], in1=r, op0=ALU.mult, op1=ALU.add
+            )
+
+        def pack_run(q):
+            nc.scalar.copy(
+                out=r_packed[q][:].rearrange("p (c i t) -> p c t i", i=4, t=SLOTS),
+                in_=r_tiles[q][:].rearrange("p t (c i) -> p c t i", i=4),
+            )
+
+        def emit_run(q, share):
+            s, c, h = run_of(q)
+            for jj in range(TILES):
+                bank = psum.tile([P, SLOTS, P], F32, name="bank", tag="bank")
+                for t in range(SLOTS):
+                    nc.tensor.transpose(bank[:, t, :], r_tiles[q][:, t, jj * P : (jj + 1) * P], ident[:])
+                rows = stage_out.tile([P, P, SLOTS], F32, name="rows", tag="rows")
+                src = bank[:].rearrange("p t m -> p m t")
+                if share and jj % 2 == 1:
+                    nc.vector.tensor_copy(out=rows[:], in_=src)
+                else:
+                    nc.scalar.copy(out=rows[:], in_=src)
+                f0 = c * CHUNK + jj * P
+                nc.sync.dma_start(
+                    out=out[f0 : f0 + P, GROUP * h : GROUP * (h + 1)], in_=rows[:].rearrange("p m t -> p (m t)")
+                )
+
+        negate(0)
+        open_run(0, True)
+        for j in range(TILES):
+            turn_x(j)
+            pack_x(j)
+        sort_weights(0, 0)
+        sort_weights(0, 1)
+        quantize_x(0)
+        turn_x(4)
+        turn_x(5)
+        for t in range(SLOTS):
+            carry(0, t, True)
+        pack_x(4)
+        pack_x(5)
+
+        last_stage = RUNS - CHUNKS * GROUPS
+        for q in range(RUNS):
+            if q + 1 < RUNS:
+                open_run(q + 1, False)
+                for t in range(SLOTS - 1):
+                    carry(q + 1, t, False)
+                if q != 0:
+                    carry(q + 1, SLOTS - 1, True)
+            for t in range(SLOTS):
+                step(q, t)
+                if t == 1 and q > last_stage:
+                    emit_run(q - 1, q == RUNS - 1)
+            if q == 0:
+                turn_x(6)
+                turn_x(7)
+                pack_x(6)
+                pack_x(7)
+                carry(1, SLOTS - 1, True)
+            if q < last_stage:
+                pack_run(q)
+            if q in (1, 5):
+                negate(1 + q // 4)
+            if 1 <= q <= last_stage:
+                quantize_run(q - 1)
+            if q in (0, 2, 4, 6):
+                sort_weights(1 + q // 4, (q // 2) % 2)
+            if q == 0:
+                quantize_x(1)
+        emit_run(RUNS - 1, True)

@@ -49,11 +49,14 @@ def tile_three_mirror_correction_t2_kernel(
         x_rows = [new("x_rows%d" % j, [P, MODES], BF16) for j in range(FRAMES // P)]
         raw_codes = {(s, h): new("raw_codes%d%d" % (s, h), [P, GROUPS, 2 * GROUP], U8) for s in range(STAGES) for h in range(GROUPS)}
         raw_scales = [new("raw_scales%d" % s, [P, GROUPS, MODES], U8) for s in range(STAGES)]
-        w_codes = {(s, h): new("w_codes%d%d" % (s, h), [P, GROUPS, SLOTS, 2 * P], U8) for s in range(STAGES) for h in range(GROUPS)}
-        w_scales = {(s, h): new("w_scales%d%d" % (s, h), [P, GROUPS, SLOTS, P], U8) for s in range(STAGES) for h in range(GROUPS)}
+        sorted_parts = [(0, 0), (0, 1), (1, 0), (1, 1), (2, 0)]
+        w_codes = {(s, h): new("w_codes%d%d" % (s, h), [P, GROUPS, SLOTS, 2 * P], U8) for s, h in sorted_parts}
+        w_scales = {(s, h): new("w_scales%d%d" % (s, h), [P, GROUPS, SLOTS, P], U8) for s, h in sorted_parts}
+        v3_row = new("v3_row", [P, GROUP], BF16)
+        r2_rows = {(c, jj): new("r2_rows%d%d" % (c, jj), [P, P, SLOTS], F32) for c in range(CHUNKS) for jj in range(TILES)}
         v_raw = [new("v_raw%d" % s, [P, GROUPS, SLOTS], BF16) for s in range(STAGES)]
         v_neg = [new("v_neg%d" % s, [P, GROUPS, SLOTS], F32) for s in range(STAGES)]
-        v_run = [new("v_run%d" % q, [P, SLOTS], F32) for q in range(RUNS)]
+        v_run = {q: new("v_run%d" % q, [P, SLOTS], F32) for q in list(range(9)) + [10]}
         x_packed = [new("x_packed%d" % c, [P, GROUPS, CHUNK * SLOTS], BF16) for c in range(CHUNKS)]
         r_packed = [new("r_packed%d" % q, [P, CHUNK * SLOTS], BF16) for q in range(RUNS - CHUNKS * GROUPS)]
         a_codes = {(s, c, g): new("a_codes%d%d%d" % (s, c, g), [P, CHUNK], U32) for s in range(STAGES) for c in range(CHUNKS) for g in range(GROUPS)}
@@ -99,6 +102,7 @@ def tile_three_mirror_correction_t2_kernel(
             load_scales(s)
             load_codes(s, 0)
             load_codes(s, 1)
+        nc.sync.dma_start(out=v3_row[:], in_=v3[GROUP : 2 * GROUP].partition_broadcast(P))
 
         def negate(s):
             nc.scalar.activation(out=v_neg[s][:], in_=v_raw[s][:], func=COPY, scale=-1.0)
@@ -179,26 +183,67 @@ def tile_three_mirror_correction_t2_kernel(
 
         def pack_run(q):
             nc.scalar.copy(
-                out=r_packed[q][:].rearrange("p (c i t) -> p c t i", i=4, t=SLOTS),
-                in_=r_tiles[q][:].rearrange("p t (c i) -> p c t i", i=4),
+                out=r_packed[q][:].rearrange("p (c i t) -> p c t i", i=2, t=SLOTS),
+                in_=r_tiles[q][:].rearrange("p t (c i) -> p c t i", i=2),
             )
 
-        def emit_run(q, share):
-            s, c, h = run_of(q)
+        def turn_run(q):
             for jj in range(TILES):
                 bank = psum.tile([P, SLOTS, P], F32, name="bank", tag="bank")
                 for t in range(SLOTS):
                     nc.tensor.transpose(bank[:, t, :], r_tiles[q][:, t, jj * P : (jj + 1) * P], ident[:])
-                rows = stage_out.tile([P, P, SLOTS], F32, name="rows", tag="rows")
-                src = bank[:].rearrange("p t m -> p m t")
-                if share and jj % 2 == 1:
-                    nc.vector.tensor_copy(out=rows[:], in_=src)
-                else:
-                    nc.scalar.copy(out=rows[:], in_=src)
-                f0 = c * CHUNK + jj * P
-                nc.sync.dma_start(
-                    out=out[f0 : f0 + P, GROUP * h : GROUP * (h + 1)], in_=rows[:].rearrange("p m t -> p (m t)")
+                banks["r", q, jj] = bank
+
+        def unload(q, jj, rows):
+            nc.scalar.copy(out=rows[:], in_=banks["r", q, jj][:].rearrange("p t m -> p m t"))
+
+        def store(c, jj, h, rows):
+            f0 = c * CHUNK + jj * P
+            nc.sync.dma_start(out=out[f0 : f0 + P, GROUP * h : GROUP * (h + 1)], in_=rows[:].rearrange("p m t -> p (m t)"))
+
+        def keep_r2_rows(q):
+            turn_run(q)
+            for jj in range(TILES):
+                unload(q, jj, r2_rows[run_of(q)[1], jj])
+
+        def row_step(c, jj):
+            bank = psum.tile([P, GROUP], F32, name="bank", tag="bank")
+            for g in range(GROUPS):
+                nc.tensor.matmul_mx(
+                    out=bank[:],
+                    lhsT=a_codes[2, c, g][:, jj * P : (jj + 1) * P].bitcast(FP8X4),
+                    lhsT_scale=a_scales[2, c, g][:, jj * P : (jj + 1) * P],
+                    rhs=raw_codes[2, 1][:, g, :].bitcast(FP4X4),
+                    rhs_scale=raw_scales[2][:, g, GROUP : 2 * GROUP],
+                    start=(g == 0),
+                    stop=(g == GROUPS - 1),
                 )
+            rows = r2_rows[c, jj][:].rearrange("p m t -> p (m t)")
+            nc.vector.tensor_tensor(out=rows, in0=rows, in1=bank[:], op=ALU.subtract)
+
+        def row_scale(c, jj):
+            rows = r2_rows[c, jj][:].rearrange("p m t -> p (m t)")
+            if jj == 0:
+                nc.gpsimd.tensor_tensor(out=rows, in0=rows, in1=v3_row[:], op=ALU.mult)
+            else:
+                nc.vector.tensor_tensor(out=rows, in0=rows, in1=v3_row[:], op=ALU.mult)
+
+        def row_run(c):
+            q = 8 + 2 * c
+            for jj in range(TILES):
+                row_step(c, jj)
+            turn_run(q)
+            for jj in range(TILES):
+                rows = stage_out.tile([P, P, SLOTS], F32, name="rows", tag="rows")
+                unload(q, jj, rows)
+                store(c, jj, 0, rows)
+                row_scale(c, jj)
+                store(c, jj, 1, r2_rows[c, jj])
+
+        def carry_ahead(q):
+            open_run(q, False)
+            for t in range(SLOTS - 1):
+                carry(q, t, False)
 
         negate(0)
         open_run(0, True)
@@ -215,32 +260,39 @@ def tile_three_mirror_correction_t2_kernel(
         pack_x(4)
         pack_x(5)
 
-        last_stage = RUNS - CHUNKS * GROUPS
-        for q in range(RUNS):
-            if q + 1 < RUNS:
-                open_run(q + 1, False)
-                for t in range(SLOTS - 1):
-                    carry(q + 1, t, False)
-                if q != 0:
-                    carry(q + 1, SLOTS - 1, True)
+        for q in range(8):
+            carry_ahead(q + 1)
+            if q != 0:
+                carry(q + 1, SLOTS - 1, True)
             for t in range(SLOTS):
                 step(q, t)
-                if t == 1 and q > last_stage:
-                    emit_run(q - 1, q == RUNS - 1)
             if q == 0:
                 turn_x(6)
                 turn_x(7)
                 pack_x(6)
                 pack_x(7)
                 carry(1, SLOTS - 1, True)
-            if q < last_stage:
-                pack_run(q)
-            if q in (1, 5):
+            pack_run(q)
+            if q in (1, 4):
                 negate(1 + q // 4)
-            if 1 <= q <= last_stage:
+            if q == 5:
+                keep_r2_rows(q)
+            if q >= 1:
                 quantize_run(q - 1)
-            if q in (0, 2, 4, 6):
-                sort_weights(1 + q // 4, (q // 2) % 2)
+            if q in (0, 2):
+                sort_weights(1, q // 2)
+            if q == 5:
+                sort_weights(2, 0)
             if q == 0:
                 quantize_x(1)
-        emit_run(RUNS - 1, True)
+
+        carry_ahead(10)
+        for t in range(SLOTS):
+            step(8, t)
+        keep_r2_rows(7)
+        carry(10, SLOTS - 1, True)
+        quantize_run(7)
+        row_run(0)
+        for t in range(SLOTS):
+            step(10, t)
+        row_run(1)

@@ -16,14 +16,16 @@ COPY = mybir.ActivationFunctionType.Copy
 P = 128
 FRAMES = 1024
 MODES = 1024
+STAGES = 3
 SLOTS = 4
 GROUP = P * SLOTS
 GROUPS = MODES // GROUP
 CHUNK = 512
 CHUNKS = FRAMES // CHUNK
 TILES = CHUNK // P
-STAGES = 3
-RUNS = STAGES * CHUNKS * GROUPS
+QUADRANT = 32
+SCALE_ROWS = GROUPS * 16
+STAGE_RUNS = CHUNKS * GROUPS
 FLOPS = STAGES * 2 * FRAMES * MODES * MODES
 
 
@@ -34,265 +36,334 @@ def tile_three_mirror_correction_t2_kernel(
     d_words = (d1_words, d2_words, d3_words)
     d_scales = (d1_scales, d2_scales, d3_scales)
     factors = (v1, v2, v3)
+    last = STAGES - 1
 
     with ExitStack() as ctx:
         keep = ctx.enter_context(tc.tile_pool(name="keep", bufs=1))
         resid = ctx.enter_context(tc.tile_pool(name="resid", bufs=2))
-        stage_out = ctx.enter_context(tc.tile_pool(name="stage_out", bufs=8))
         psum = ctx.enter_context(tc.psum_pool(name="psum", bufs=8))
         ctx.enter_context(tc.manual_schedule())
 
         def new(name, shape, dtype):
             return keep.tile(shape, dtype, name=name, align_bytes=64)
 
+        halves = [(s, h) for s in range(STAGES) for h in range(GROUPS)]
+        sorted_halves = halves[:-1]
+        operands = [(s, c, g) for s in range(STAGES) for c in range(CHUNKS) for g in range(GROUPS)]
+        frame_tiles = [(c, j) for c in range(CHUNKS) for j in range(TILES)]
+
         ident = new("ident", [P, P], F32)
-        x_rows = [new("x_rows%d" % j, [P, MODES], BF16) for j in range(FRAMES // P)]
-        raw_codes = {(s, h): new("raw_codes%d%d" % (s, h), [P, GROUPS, 2 * GROUP], U8) for s in range(STAGES) for h in range(GROUPS)}
-        raw_scales = [new("raw_scales%d" % s, [P, GROUPS, MODES], U8) for s in range(STAGES)]
-        sorted_parts = [(0, 0), (0, 1), (1, 0), (1, 1), (2, 0)]
-        w_codes = {(s, h): new("w_codes%d%d" % (s, h), [P, GROUPS, SLOTS, 2 * P], U8) for s, h in sorted_parts}
-        w_scales = {(s, h): new("w_scales%d%d" % (s, h), [P, GROUPS, SLOTS, P], U8) for s, h in sorted_parts}
-        v3_row = new("v3_row", [P, GROUP], BF16)
-        r2_rows = {(c, jj): new("r2_rows%d%d" % (c, jj), [P, P, SLOTS], F32) for c in range(CHUNKS) for jj in range(TILES)}
+        x_rows = {(c, j): new("x_rows%d%d" % (c, j), [P, MODES], BF16) for c, j in frame_tiles}
+        raw_codes = {(s, h): new("raw_codes%d%d" % (s, h), [P, GROUPS, 2 * GROUP], U8) for s, h in halves}
+        w_codes = {(s, h): new("w_codes%d%d" % (s, h), [P, GROUPS, SLOTS, 2 * P], U8) for s, h in sorted_halves}
+        flat_scales = new("flat_scales", [P, MODES], U8)
+        flat_sorted = new("flat_sorted", [P, GROUPS, SLOTS, P], U8)
+        w_scales = [new("w_scales%d" % s, [P, GROUPS, GROUPS, SLOTS, P], U8) for s in range(STAGES)]
+        row_scales = new("row_scales", [P, GROUPS, GROUP], U8)
         v_raw = [new("v_raw%d" % s, [P, GROUPS, SLOTS], BF16) for s in range(STAGES)]
+        v_pos = [new("v_pos%d" % s, [P, GROUPS, SLOTS], F32) for s in range(last)]
         v_neg = [new("v_neg%d" % s, [P, GROUPS, SLOTS], F32) for s in range(STAGES)]
-        v_run = {q: new("v_run%d" % q, [P, SLOTS], F32) for q in list(range(9)) + [10]}
+        v3_row = new("v3_row", [P, GROUP], BF16)
         x_packed = [new("x_packed%d" % c, [P, GROUPS, CHUNK * SLOTS], BF16) for c in range(CHUNKS)]
-        r_packed = [new("r_packed%d" % q, [P, CHUNK * SLOTS], BF16) for q in range(RUNS - CHUNKS * GROUPS)]
-        a_codes = {(s, c, g): new("a_codes%d%d%d" % (s, c, g), [P, CHUNK], U32) for s in range(STAGES) for c in range(CHUNKS) for g in range(GROUPS)}
-        a_scales = {(s, c, g): new("a_scales%d%d%d" % (s, c, g), [P, CHUNK], U8) for s in range(STAGES) for c in range(CHUNKS) for g in range(GROUPS)}
+        r_packed = [new("r_packed%d" % q, [P, CHUNK * SLOTS], BF16) for q in range(last * STAGE_RUNS)]
+        a_codes = {key: new("a_codes%d%d%d" % key, [P, CHUNK], U32) for key in operands}
+        a_scales = {key: new("a_scales%d%d%d" % key, [P, CHUNK], U8) for key in operands}
+        lower_rows = {(c, j): new("lower_rows%d%d" % (c, j), [P, P, SLOTS], F32) for c, j in frame_tiles}
+        upper_rows = {(c, j): new("upper_rows%d%d" % (c, j), [P, P, SLOTS], F32) for c, j in frame_tiles}
         r_tiles = {}
         banks = {}
 
         def run_of(q):
-            return q // (CHUNKS * GROUPS), (q // GROUPS) % CHUNKS, q % GROUPS
+            return q // STAGE_RUNS, (q // GROUPS) % CHUNKS, q % GROUPS
 
-        def load_x(j):
-            nc.sync.dma_start(out=x_rows[j][:], in_=x[j * P : (j + 1) * P, :])
+        def load_x(c, j):
+            f0 = c * CHUNK + j * P
+            nc.sync.dma_start(out=x_rows[c, j][:], in_=x[f0 : f0 + P, :])
 
         def load_factor(s):
-            nc.sync.dma_start(out=v_raw[s][:], in_=factors[s].rearrange("(g p t) -> p g t", p=P, t=SLOTS))
+            nc.sync.dma_start(out=v_raw[s][:], in_=factors[s].rearrange("(h p t) -> p h t", p=P, t=SLOTS))
 
         def load_codes(s, h):
             src = d_words[s][:, :, 2 * GROUP * h : 2 * GROUP * (h + 1)].rearrange("g p n -> p g n")
             nc.sync.dma_start(out=raw_codes[s, h][:].bitcast(I32), in_=src.bitcast(I32))
 
-        def load_scales(s):
+        def load_flat_scales(s):
+            dst = flat_scales[SCALE_ROWS * s : SCALE_ROWS * (s + 1), :]
+            nc.sync.dma_start(out=dst.bitcast(I32), in_=d_scales[s].rearrange("g q n -> (g q) n").bitcast(I32))
+
+        def spread_scales(s, groups):
+            for g in range(GROUPS):
+                for quad in range(4):
+                    row = SCALE_ROWS * s + 16 * g + 4 * quad
+                    src = flat_sorted[row : row + 4, 0:groups].rearrange("p h t m -> p (h t m)")
+                    dst = w_scales[s][QUADRANT * quad : QUADRANT * quad + 4, g, 0:groups]
+                    nc.sync.dma_start(out=dst.rearrange("p h t m -> p (h t m)").bitcast(I32), in_=src.bitcast(I32))
+
+        def load_row_scales():
             for quad in range(4):
-                src = d_scales[s][:, 4 * quad : 4 * quad + 4, :].rearrange("g r n -> r g n")
-                nc.sync.dma_start(out=raw_scales[s][32 * quad : 32 * quad + 4, :, :].bitcast(I32), in_=src.bitcast(I32))
+                src = d3_scales[:, 4 * quad : 4 * quad + 4, GROUP : 2 * GROUP].rearrange("g r n -> r g n")
+                dst = row_scales[QUADRANT * quad : QUADRANT * quad + 4, :, :]
+                nc.sync.dma_start(out=dst.bitcast(I32), in_=src.bitcast(I32))
 
-        nc.vector.memset(raw_scales[0][:].bitcast(I32), 0)
+        nc.vector.memset(flat_scales[SCALE_ROWS * STAGES : P, :].bitcast(I32), 0)
+        nc.vector.memset(w_scales[0][:].rearrange("p g h t m -> p (g h t m)").bitcast(I32), 0)
         make_identity(nc, ident[:])
-        nc.gpsimd.memset(raw_scales[1][:].bitcast(I32), 0)
-        nc.gpsimd.memset(raw_scales[2][:].bitcast(I32), 0)
+        nc.gpsimd.memset(w_scales[1][:].rearrange("p g h t m -> p (g h t m)").bitcast(I32), 0)
+        nc.gpsimd.memset(w_scales[2][:, :, 0].rearrange("p g t m -> p g (t m)").bitcast(I32), 0)
+        nc.gpsimd.memset(row_scales[:].bitcast(I32), 0)
 
-        load_x(0)
+        load_x(0, 0)
         load_factor(0)
-        load_x(1)
+        for s in range(STAGES):
+            load_flat_scales(s)
         load_codes(0, 0)
-        load_x(2)
-        load_x(3)
-        load_scales(0)
+        load_x(0, 1)
+        load_x(0, 2)
         load_codes(0, 1)
-        for j in range(TILES, 2 * TILES):
-            load_x(j)
-        for s in (1, 2):
-            load_factor(s)
-            load_scales(s)
-            load_codes(s, 0)
-            load_codes(s, 1)
+        load_x(0, 3)
+        load_codes(1, 0)
+        load_x(1, 0)
+        load_x(1, 1)
+        nc.vector.tensor_copy(
+            out=flat_sorted[:], in_=flat_scales[:].rearrange("p (h m t) -> p h t m", h=GROUPS, t=SLOTS)
+        )
+        spread_scales(0, GROUPS)
+        load_codes(1, 1)
+        load_x(1, 2)
+        load_x(1, 3)
+        load_codes(2, 0)
+        load_factor(1)
+        spread_scales(1, GROUPS)
+        load_factor(2)
+        load_codes(2, 1)
+        spread_scales(2, 1)
+        load_row_scales()
         nc.sync.dma_start(out=v3_row[:], in_=v3[GROUP : 2 * GROUP].partition_broadcast(P))
 
-        def negate(s):
+        def widen_factor(s):
             nc.scalar.activation(out=v_neg[s][:], in_=v_raw[s][:], func=COPY, scale=-1.0)
+            if s < last:
+                nc.scalar.copy(out=v_pos[s][:], in_=v_raw[s][:])
 
-        def sort_weights(s, h):
+        def sort_codes(s, h):
             nc.vector.tensor_copy(
                 out=w_codes[s, h][:].rearrange("p g t (m b) -> p g t m b", b=2),
                 in_=raw_codes[s, h][:].rearrange("p g (m t b) -> p g t m b", t=SLOTS, b=2),
             )
-            nc.vector.tensor_copy(
-                out=w_scales[s, h][:],
-                in_=raw_scales[s][:, :, GROUP * h : GROUP * (h + 1)].rearrange("p g (m t) -> p g t m", t=SLOTS),
-            )
 
-        def turn_x(j):
+        def turn_x(c, j):
             bank = psum.tile([P, GROUPS, 2, P], F32, name="bank", tag="bank")
-            words = x_rows[j][:].bitcast(F32)
-            half = GROUP // 2
+            words = x_rows[c, j][:].bitcast(F32)
+            group_words = GROUP // 2
             for g in range(GROUPS):
                 for u in range(2):
-                    nc.tensor.transpose(bank[:, g, u, :], words[:, half * g + u : half * (g + 1) : 2], ident[:])
-            banks["x", j] = bank
+                    src = words[:, group_words * g + u : group_words * (g + 1) : 2]
+                    nc.tensor.transpose(bank[:, g, u, :], src, ident[:])
+            banks["x", c, j] = bank
 
-        def pack_x(j):
-            c, jj = divmod(j, TILES)
-            dst = x_packed[c][:].bitcast(F32).rearrange("p g (r u) -> p g r u", u=2)
-            nc.scalar.copy(out=dst[:, :, jj * P : (jj + 1) * P, :], in_=banks["x", j][:].rearrange("p g u r -> p g r u"))
+        def pack_x(c, j):
+            dst = x_packed[c][:].bitcast(F32).rearrange("p g (f u) -> p g f u", u=2)[:, :, j * P : (j + 1) * P, :]
+            nc.scalar.copy(out=dst, in_=banks["x", c, j][:].rearrange("p g u f -> p g f u"))
 
-        def quantize(s, c, g, src):
-            nc.vector.quantize_mx(out=a_codes[s, c, g][:].bitcast(FP8X4), scales=a_scales[s, c, g][:], in_=src)
+        def quantize(key, src):
+            nc.vector.quantize_mx(out=a_codes[key][:].bitcast(FP8X4), scales=a_scales[key][:], in_=src)
 
         def quantize_x(c):
             for g in range(GROUPS):
-                quantize(0, c, g, x_packed[c][:, g, :])
+                quantize((0, c, g), x_packed[c][:, g, :])
 
         def quantize_run(q):
             s, c, h = run_of(q)
-            quantize(s + 1, c, h, r_packed[q][:])
+            quantize((s + 1, c, h), r_packed[q][:])
 
-        def open_run(q, on_scalar):
+        def carry_operands(q, t):
             s, c, h = run_of(q)
-            r_tiles[q] = resid.tile([P, SLOTS, CHUNK], F32, name="r%d%d" % (c, h), tag="r%d%d" % (c, h))
-            if on_scalar:
-                nc.scalar.copy(out=v_run[q][:], in_=v_raw[s][:, h, :])
-            else:
-                nc.vector.tensor_copy(out=v_run[q][:], in_=v_raw[s][:, h, :])
-
-        def carry(q, t, on_scalar):
-            s, c, h = run_of(q)
+            if q not in r_tiles:
+                r_tiles[q] = resid.tile([P, SLOTS, CHUNK], F32, name="r%d%d" % (c, h), tag="r%d%d" % (c, h))
             if s == 0:
-                src = x_packed[c][:, h, :].rearrange("p (n t) -> p t n", t=SLOTS)[:, t, :]
+                src = x_packed[c][:, h, :].rearrange("p (f t) -> p t f", t=SLOTS)[:, t, :]
             else:
-                src = r_tiles[q - CHUNKS * GROUPS][:, t, :]
-            dst = r_tiles[q][:, t, :]
-            factor = v_run[q][:, t : t + 1]
-            if on_scalar:
-                nc.scalar.activation(out=dst, in_=src, func=COPY, scale=factor)
-            else:
-                nc.gpsimd.tensor_scalar(out=dst, in0=src, scalar1=factor, scalar2=0.0, op0=ALU.mult, op1=ALU.add)
+                src = r_tiles[q - STAGE_RUNS][:, t, :]
+            return r_tiles[q][:, t, :], src
 
-        def step(q, t):
+        def carry_on_scalar(q, slots):
             s, c, h = run_of(q)
-            bank = psum.tile([P, CHUNK], F32, name="bank", tag="bank")
-            for g in range(GROUPS):
-                nc.tensor.matmul_mx(
-                    out=bank[:],
-                    lhsT=w_codes[s, h][:, g, t, :].bitcast(FP4X4),
-                    lhsT_scale=w_scales[s, h][:, g, t, :],
-                    rhs=a_codes[s, c, g][:].bitcast(FP8X4),
-                    rhs_scale=a_scales[s, c, g][:],
-                    start=(g == 0),
-                    stop=(g == GROUPS - 1),
-                )
+            for t in slots:
+                dst, src = carry_operands(q, t)
+                nc.scalar.activation(out=dst, in_=src, func=COPY, scale=v_pos[s][:, h, t : t + 1])
+
+        def carry_on_gpsimd(jobs):
+            s = run_of(jobs[0][0])[0]
+            factor = new("v_gpsimd%d" % jobs[0][0], [P, GROUPS, SLOTS], F32)
+            nc.vector.tensor_copy(out=factor[:], in_=v_raw[s][:])
+            for q, count in jobs:
+                for t in range(count):
+                    dst, src = carry_operands(q, t)
+                    scalar = factor[:, run_of(q)[2], t : t + 1]
+                    nc.gpsimd.tensor_scalar(out=dst, in0=src, scalar1=scalar, scalar2=0.0, op0=ALU.mult, op1=ALU.add)
+
+        def multiply(q, t, g):
+            s, c, h = run_of(q)
+            if g == 0:
+                banks["mm", q, t] = psum.tile([P, CHUNK], F32, name="bank", tag="bank")
+            nc.tensor.matmul_mx(
+                out=banks["mm", q, t][:],
+                lhsT=w_codes[s, h][:, g, t, :].bitcast(FP4X4),
+                lhsT_scale=w_scales[s][:, g, h, t, :],
+                rhs=a_codes[s, c, g][:].bitcast(FP8X4),
+                rhs_scale=a_scales[s, c, g][:],
+                start=(g == 0),
+                stop=(g == GROUPS - 1),
+            )
+
+        def correct(q, t):
+            s, c, h = run_of(q)
             r = r_tiles[q][:, t, :]
             nc.vector.scalar_tensor_tensor(
-                out=r, in0=bank[:], scalar=v_neg[s][:, h, t : t + 1], in1=r, op0=ALU.mult, op1=ALU.add
+                out=r, in0=banks["mm", q, t][:], scalar=v_neg[s][:, h, t : t + 1], in1=r, op0=ALU.mult, op1=ALU.add
             )
+
+        def steps(q, slots=range(SLOTS)):
+            for t in slots:
+                for g in range(GROUPS):
+                    multiply(q, t, g)
+                correct(q, t)
 
         def pack_run(q):
             nc.scalar.copy(
-                out=r_packed[q][:].rearrange("p (c i t) -> p c t i", i=2, t=SLOTS),
-                in_=r_tiles[q][:].rearrange("p t (c i) -> p c t i", i=2),
+                out=r_packed[q][:].rearrange("p (f i t) -> p f t i", i=2, t=SLOTS),
+                in_=r_tiles[q][:].rearrange("p t (f i) -> p f t i", i=2),
             )
 
         def turn_run(q):
-            for jj in range(TILES):
+            for j in range(TILES):
                 bank = psum.tile([P, SLOTS, P], F32, name="bank", tag="bank")
                 for t in range(SLOTS):
-                    nc.tensor.transpose(bank[:, t, :], r_tiles[q][:, t, jj * P : (jj + 1) * P], ident[:])
-                banks["r", q, jj] = bank
+                    nc.tensor.transpose(bank[:, t, :], r_tiles[q][:, t, j * P : (j + 1) * P], ident[:])
+                banks["r", q, j] = bank
 
-        def unload(q, jj, rows):
-            nc.scalar.copy(out=rows[:], in_=banks["r", q, jj][:].rearrange("p t m -> p m t"))
+        def unload(q, j, rows):
+            nc.scalar.copy(out=rows[:], in_=banks["r", q, j][:].rearrange("f t m -> f m t"))
 
-        def store(c, jj, h, rows):
-            f0 = c * CHUNK + jj * P
-            nc.sync.dma_start(out=out[f0 : f0 + P, GROUP * h : GROUP * (h + 1)], in_=rows[:].rearrange("p m t -> p (m t)"))
+        def store(c, j, h, rows):
+            f0 = c * CHUNK + j * P
+            dst = out[f0 : f0 + P, GROUP * h : GROUP * (h + 1)]
+            nc.sync.dma_start(out=dst, in_=rows[:].rearrange("f m t -> f (m t)"))
 
-        def keep_r2_rows(q):
+        def turn_upper_r2(c):
+            q = STAGE_RUNS + GROUPS * c + 1
             turn_run(q)
-            for jj in range(TILES):
-                unload(q, jj, r2_rows[run_of(q)[1], jj])
+            for j in range(TILES):
+                unload(q, j, upper_rows[c, j])
 
-        def row_step(c, jj):
+        def emit_lower(c, j):
+            unload(last * STAGE_RUNS + GROUPS * c, j, lower_rows[c, j])
+            store(c, j, 0, lower_rows[c, j])
+
+        def row_subtract(c, j):
             bank = psum.tile([P, GROUP], F32, name="bank", tag="bank")
             for g in range(GROUPS):
                 nc.tensor.matmul_mx(
                     out=bank[:],
-                    lhsT=a_codes[2, c, g][:, jj * P : (jj + 1) * P].bitcast(FP8X4),
-                    lhsT_scale=a_scales[2, c, g][:, jj * P : (jj + 1) * P],
-                    rhs=raw_codes[2, 1][:, g, :].bitcast(FP4X4),
-                    rhs_scale=raw_scales[2][:, g, GROUP : 2 * GROUP],
+                    lhsT=a_codes[last, c, g][:, j * P : (j + 1) * P].bitcast(FP8X4),
+                    lhsT_scale=a_scales[last, c, g][:, j * P : (j + 1) * P],
+                    rhs=raw_codes[last, 1][:, g, :].bitcast(FP4X4),
+                    rhs_scale=row_scales[:, g, :],
                     start=(g == 0),
                     stop=(g == GROUPS - 1),
                 )
-            rows = r2_rows[c, jj][:].rearrange("p m t -> p (m t)")
+            rows = upper_rows[c, j][:].rearrange("f m t -> f (m t)")
             nc.vector.tensor_tensor(out=rows, in0=rows, in1=bank[:], op=ALU.subtract)
 
-        def row_scale(c, jj):
-            rows = r2_rows[c, jj][:].rearrange("p m t -> p (m t)")
-            if jj == 0:
-                nc.gpsimd.tensor_tensor(out=rows, in0=rows, in1=v3_row[:], op=ALU.mult)
-            else:
-                nc.vector.tensor_tensor(out=rows, in0=rows, in1=v3_row[:], op=ALU.mult)
+        def row_scale(c, j, engine):
+            rows = upper_rows[c, j][:].rearrange("f m t -> f (m t)")
+            engine.tensor_tensor(out=rows, in0=rows, in1=v3_row[:], op=ALU.mult)
 
-        def row_run(c):
-            q = 8 + 2 * c
-            for jj in range(TILES):
-                row_step(c, jj)
-            turn_run(q)
-            for jj in range(TILES):
-                rows = stage_out.tile([P, P, SLOTS], F32, name="rows", tag="rows")
-                unload(q, jj, rows)
-                store(c, jj, 0, rows)
-                row_scale(c, jj)
-                store(c, jj, 1, r2_rows[c, jj])
+        def emit_upper(c, j, engine):
+            row_scale(c, j, engine)
+            store(c, j, 1, upper_rows[c, j])
 
-        def carry_ahead(q):
-            open_run(q, False)
-            for t in range(SLOTS - 1):
-                carry(q, t, False)
-
-        negate(0)
-        open_run(0, True)
+        widen_factor(0)
         for j in range(TILES):
-            turn_x(j)
-            pack_x(j)
-        sort_weights(0, 0)
-        sort_weights(0, 1)
+            turn_x(0, j)
+            pack_x(0, j)
+        sort_codes(0, 0)
+        sort_codes(0, 1)
+        sort_codes(1, 0)
         quantize_x(0)
-        turn_x(4)
-        turn_x(5)
-        for t in range(SLOTS):
-            carry(0, t, True)
-        pack_x(4)
-        pack_x(5)
-
-        for q in range(8):
-            carry_ahead(q + 1)
-            if q != 0:
-                carry(q + 1, SLOTS - 1, True)
-            for t in range(SLOTS):
-                step(q, t)
-            if q == 0:
-                turn_x(6)
-                turn_x(7)
-                pack_x(6)
-                pack_x(7)
-                carry(1, SLOTS - 1, True)
+        turn_x(1, 0)
+        turn_x(1, 1)
+        carry_on_scalar(0, range(SLOTS))
+        pack_x(1, 0)
+        pack_x(1, 1)
+        sort_codes(1, 1)
+        carry_on_gpsimd([(1, 1)])
+        steps(0, (0, 1))
+        for j in (2, 3):
+            turn_x(1, j)
+            pack_x(1, j)
+        carry_on_scalar(1, (1, 2, 3))
+        sort_codes(2, 0)
+        quantize_x(1)
+        carry_on_gpsimd([(2, 3), (3, 3)])
+        carry_on_scalar(2, (3,))
+        carry_on_scalar(3, (3,))
+        widen_factor(1)
+        steps(0, (2, 3))
+        pack_run(0)
+        for q in (1, 2):
+            steps(q)
             pack_run(q)
-            if q in (1, 4):
-                negate(1 + q // 4)
-            if q == 5:
-                keep_r2_rows(q)
-            if q >= 1:
-                quantize_run(q - 1)
-            if q in (0, 2):
-                sort_weights(1, q // 2)
-            if q == 5:
-                sort_weights(2, 0)
-            if q == 0:
-                quantize_x(1)
+        quantize_run(0)
+        quantize_run(1)
 
-        carry_ahead(10)
-        for t in range(SLOTS):
-            step(8, t)
-        keep_r2_rows(7)
-        carry(10, SLOTS - 1, True)
+        for q in (3, 5):
+            carry_on_gpsimd([(q + 1, 3), (q + 2, 2)])
+            carry_on_scalar(q + 1, (3,))
+            steps(q)
+            pack_run(q)
+            carry_on_scalar(q + 2, (2, 3))
+            steps(q + 1)
+            if q == STAGE_RUNS + 1:
+                turn_upper_r2(0)
+            else:
+                widen_factor(last)
+            pack_run(q + 1)
+            quantize_run(q - 1)
+            quantize_run(q)
+
+        carry_on_gpsimd([(8, SLOTS), (10, SLOTS)])
+        steps(7)
+        pack_run(7)
+        steps(8)
+        for j in range(TILES - 1):
+            row_subtract(0, j)
+        quantize_run(6)
         quantize_run(7)
-        row_run(0)
-        for t in range(SLOTS):
-            step(10, t)
-        row_run(1)
+        turn_run(8)
+        row_subtract(0, TILES - 1)
+        for j in range(TILES):
+            emit_lower(0, j)
+        emit_upper(0, TILES - 1, nc.gpsimd)
+        for g in range(GROUPS):
+            for t in range(SLOTS - 1):
+                multiply(10, t, g)
+        for t in range(SLOTS - 1):
+            correct(10, t)
+        steps(10, (SLOTS - 1,))
+        turn_upper_r2(1)
+        emit_upper(0, 0, nc.gpsimd)
+        emit_upper(0, 1, nc.vector)
+        emit_upper(0, 2, nc.vector)
+        row_subtract(1, 0)
+        row_subtract(1, 1)
+        turn_run(10)
+        for j in (0, 1):
+            emit_lower(1, j)
+            emit_upper(1, j, nc.vector)
+        for j in (2, 3):
+            emit_lower(1, j)
+        for j in (2, 3):
+            row_subtract(1, j)
+        for j in (2, 3):
+            emit_upper(1, j, nc.vector)

@@ -231,8 +231,8 @@ def tile_three_mirror_correction_t2_kernel(
 
         def pack_run(q):
             nc.scalar.copy(
-                out=r_packed[q][:].rearrange("p (f i t) -> p f t i", i=2, t=SLOTS),
-                in_=r_tiles[q][:].rearrange("p t (f i) -> p f t i", i=2),
+                out=r_packed[q][:].rearrange("p (f i t) -> p f t i", i=4, t=SLOTS),
+                in_=r_tiles[q][:].rearrange("p t (f i) -> p f t i", i=4),
             )
 
         def turn_run(q):

from contextlib import ExitStack

import concourse.mybir as mybir
from concourse.masks import make_identity

F32 = mybir.dt.float32
BF16 = mybir.dt.bfloat16
I32 = mybir.dt.int32
U32 = mybir.dt.uint32
U8 = mybir.dt.uint8
FP8X4 = mybir.dt.float8_e4m3fn_x4
FP4X4 = mybir.dt.float4_e2m1fn_x4
ALU = mybir.AluOpType
COPY = mybir.ActivationFunctionType.Copy

P = 128
FRAMES = 1024
MODES = 1024
STAGES = 3
SLOTS = 4
GROUP = P * SLOTS
GROUPS = MODES // GROUP
CHUNK = 512
CHUNKS = FRAMES // CHUNK
TILES = CHUNK // P
QUADRANT = 32
SCALE_ROWS = GROUPS * 16
STAGE_RUNS = CHUNKS * GROUPS
FLOPS = STAGES * 2 * FRAMES * MODES * MODES


def tile_three_mirror_correction_t2_kernel(
    tc, x, d1_words, d1_scales, d2_words, d2_scales, d3_words, d3_scales, v1, v2, v3, out
):
    nc = tc.nc
    d_words = (d1_words, d2_words, d3_words)
    d_scales = (d1_scales, d2_scales, d3_scales)
    factors = (v1, v2, v3)
    last = STAGES - 1

    with ExitStack() as ctx:
        keep = ctx.enter_context(tc.tile_pool(name="keep", bufs=1))
        resid = ctx.enter_context(tc.tile_pool(name="resid", bufs=2))
        psum = ctx.enter_context(tc.psum_pool(name="psum", bufs=8))
        ctx.enter_context(tc.manual_schedule())

        def new(name, shape, dtype):
            return keep.tile(shape, dtype, name=name, align_bytes=64)

        halves = [(s, h) for s in range(STAGES) for h in range(GROUPS)]
        sorted_halves = halves[:-1]
        operands = [(s, c, g) for s in range(STAGES) for c in range(CHUNKS) for g in range(GROUPS)]
        frame_tiles = [(c, j) for c in range(CHUNKS) for j in range(TILES)]

        ident = new("ident", [P, P], F32)
        x_rows = {(c, j): new("x_rows%d%d" % (c, j), [P, MODES], BF16) for c, j in frame_tiles}
        raw_codes = {(s, h): new("raw_codes%d%d" % (s, h), [P, GROUPS, 2 * GROUP], U8) for s, h in halves}
        w_codes = {(s, h): new("w_codes%d%d" % (s, h), [P, GROUPS, SLOTS, 2 * P], U8) for s, h in sorted_halves}
        flat_scales = new("flat_scales", [P, MODES], U8)
        flat_sorted = new("flat_sorted", [P, GROUPS, SLOTS, P], U8)
        w_scales = [new("w_scales%d" % s, [P, GROUPS, GROUPS, SLOTS, P], U8) for s in range(STAGES)]
        row_scales = new("row_scales", [P, GROUPS, GROUP], U8)
        v_raw = [new("v_raw%d" % s, [P, GROUPS, SLOTS], BF16) for s in range(STAGES)]
        v_pos = [new("v_pos%d" % s, [P, GROUPS, SLOTS], F32) for s in range(last)]
        v_neg = [new("v_neg%d" % s, [P, GROUPS, SLOTS], F32) for s in range(STAGES)]
        v3_row = new("v3_row", [P, GROUP], BF16)
        x_packed = [new("x_packed%d" % c, [P, GROUPS, CHUNK * SLOTS], BF16) for c in range(CHUNKS)]
        r_packed = [new("r_packed%d" % q, [P, CHUNK * SLOTS], BF16) for q in range(last * STAGE_RUNS)]
        a_codes = {key: new("a_codes%d%d%d" % key, [P, CHUNK], U32) for key in operands}
        a_scales = {key: new("a_scales%d%d%d" % key, [P, CHUNK], U8) for key in operands}
        lower_rows = {(c, j): new("lower_rows%d%d" % (c, j), [P, P, SLOTS], F32) for c, j in frame_tiles}
        upper_rows = {(c, j): new("upper_rows%d%d" % (c, j), [P, P, SLOTS], F32) for c, j in frame_tiles}
        r_tiles = {}
        banks = {}

        def run_of(q):
            return q // STAGE_RUNS, (q // GROUPS) % CHUNKS, q % GROUPS

        def load_x(c, j):
            f0 = c * CHUNK + j * P
            nc.sync.dma_start(out=x_rows[c, j][:], in_=x[f0 : f0 + P, :])

        def load_factor(s):
            nc.sync.dma_start(out=v_raw[s][:], in_=factors[s].rearrange("(h p t) -> p h t", p=P, t=SLOTS))

        def load_codes(s, h):
            src = d_words[s][:, :, 2 * GROUP * h : 2 * GROUP * (h + 1)].rearrange("g p n -> p g n")
            nc.sync.dma_start(out=raw_codes[s, h][:].bitcast(I32), in_=src.bitcast(I32))

        def load_flat_scales(s):
            dst = flat_scales[SCALE_ROWS * s : SCALE_ROWS * (s + 1), :]
            nc.sync.dma_start(out=dst.bitcast(I32), in_=d_scales[s].rearrange("g q n -> (g q) n").bitcast(I32))

        def spread_scales(s, groups):
            for g in range(GROUPS):
                for quad in range(4):
                    row = SCALE_ROWS * s + 16 * g + 4 * quad
                    src = flat_sorted[row : row + 4, 0:groups].rearrange("p h t m -> p (h t m)")
                    dst = w_scales[s][QUADRANT * quad : QUADRANT * quad + 4, g, 0:groups]
                    nc.sync.dma_start(out=dst.rearrange("p h t m -> p (h t m)").bitcast(I32), in_=src.bitcast(I32))

        def load_row_scales():
            for quad in range(4):
                src = d3_scales[:, 4 * quad : 4 * quad + 4, GROUP : 2 * GROUP].rearrange("g r n -> r g n")
                dst = row_scales[QUADRANT * quad : QUADRANT * quad + 4, :, :]
                nc.sync.dma_start(out=dst.bitcast(I32), in_=src.bitcast(I32))

        nc.vector.memset(flat_scales[SCALE_ROWS * STAGES : P, :].bitcast(I32), 0)
        nc.vector.memset(w_scales[0][:].rearrange("p g h t m -> p (g h t m)").bitcast(I32), 0)
        make_identity(nc, ident[:])
        nc.gpsimd.memset(w_scales[1][:].rearrange("p g h t m -> p (g h t m)").bitcast(I32), 0)
        nc.gpsimd.memset(w_scales[2][:, :, 0].rearrange("p g t m -> p g (t m)").bitcast(I32), 0)
        nc.gpsimd.memset(row_scales[:].bitcast(I32), 0)

        load_x(0, 0)
        load_factor(0)
        for s in range(STAGES):
            load_flat_scales(s)
        load_codes(0, 0)
        load_x(0, 1)
        load_x(0, 2)
        load_codes(0, 1)
        load_x(0, 3)
        load_codes(1, 0)
        load_x(1, 0)
        load_x(1, 1)
        nc.vector.tensor_copy(
            out=flat_sorted[:], in_=flat_scales[:].rearrange("p (h m t) -> p h t m", h=GROUPS, t=SLOTS)
        )
        spread_scales(0, GROUPS)
        load_codes(1, 1)
        load_x(1, 2)
        load_x(1, 3)
        load_codes(2, 0)
        load_factor(1)
        spread_scales(1, GROUPS)
        load_factor(2)
        load_codes(2, 1)
        spread_scales(2, 1)
        load_row_scales()
        nc.sync.dma_start(out=v3_row[:], in_=v3[GROUP : 2 * GROUP].partition_broadcast(P))

        def widen_factor(s):
            nc.scalar.activation(out=v_neg[s][:], in_=v_raw[s][:], func=COPY, scale=-1.0)
            if s < last:
                nc.scalar.copy(out=v_pos[s][:], in_=v_raw[s][:])

        def sort_codes(s, h):
            nc.vector.tensor_copy(
                out=w_codes[s, h][:].rearrange("p g t (m b) -> p g t m b", b=2),
                in_=raw_codes[s, h][:].rearrange("p g (m t b) -> p g t m b", t=SLOTS, b=2),
            )

        def turn_x(c, j):
            bank = psum.tile([P, GROUPS, 2, P], F32, name="bank", tag="bank")
            words = x_rows[c, j][:].bitcast(F32)
            group_words = GROUP // 2
            for g in range(GROUPS):
                for u in range(2):
                    src = words[:, group_words * g + u : group_words * (g + 1) : 2]
                    nc.tensor.transpose(bank[:, g, u, :], src, ident[:])
            banks["x", c, j] = bank

        def pack_x(c, j):
            dst = x_packed[c][:].bitcast(F32).rearrange("p g (f u) -> p g f u", u=2)[:, :, j * P : (j + 1) * P, :]
            nc.scalar.copy(out=dst, in_=banks["x", c, j][:].rearrange("p g u f -> p g f u"))

        def quantize(key, src):
            nc.vector.quantize_mx(out=a_codes[key][:].bitcast(FP8X4), scales=a_scales[key][:], in_=src)

        def quantize_x(c):
            for g in range(GROUPS):
                quantize((0, c, g), x_packed[c][:, g, :])

        def quantize_run(q):
            s, c, h = run_of(q)
            quantize((s + 1, c, h), r_packed[q][:])

        def carry_operands(q, t):
            s, c, h = run_of(q)
            if q not in r_tiles:
                r_tiles[q] = resid.tile([P, SLOTS, CHUNK], F32, name="r%d%d" % (c, h), tag="r%d%d" % (c, h))
            if s == 0:
                src = x_packed[c][:, h, :].rearrange("p (f t) -> p t f", t=SLOTS)[:, t, :]
            else:
                src = r_tiles[q - STAGE_RUNS][:, t, :]
            return r_tiles[q][:, t, :], src

        def carry_on_scalar(q, slots):
            s, c, h = run_of(q)
            for t in slots:
                dst, src = carry_operands(q, t)
                nc.scalar.activation(out=dst, in_=src, func=COPY, scale=v_pos[s][:, h, t : t + 1])

        def carry_on_gpsimd(jobs):
            s = run_of(jobs[0][0])[0]
            factor = new("v_gpsimd%d" % jobs[0][0], [P, GROUPS, SLOTS], F32)
            nc.vector.tensor_copy(out=factor[:], in_=v_raw[s][:])
            for q, count in jobs:
                for t in range(count):
                    dst, src = carry_operands(q, t)
                    scalar = factor[:, run_of(q)[2], t : t + 1]
                    nc.gpsimd.tensor_scalar(out=dst, in0=src, scalar1=scalar, scalar2=0.0, op0=ALU.mult, op1=ALU.add)

        def multiply(q, t, g):
            s, c, h = run_of(q)
            if g == 0:
                banks["mm", q, t] = psum.tile([P, CHUNK], F32, name="bank", tag="bank")
            nc.tensor.matmul_mx(
                out=banks["mm", q, t][:],
                lhsT=w_codes[s, h][:, g, t, :].bitcast(FP4X4),
                lhsT_scale=w_scales[s][:, g, h, t, :],
                rhs=a_codes[s, c, g][:].bitcast(FP8X4),
                rhs_scale=a_scales[s, c, g][:],
                start=(g == 0),
                stop=(g == GROUPS - 1),
            )

        def correct(q, t):
            s, c, h = run_of(q)
            r = r_tiles[q][:, t, :]
            nc.vector.scalar_tensor_tensor(
                out=r, in0=banks["mm", q, t][:], scalar=v_neg[s][:, h, t : t + 1], in1=r, op0=ALU.mult, op1=ALU.add
            )

        def steps(q, slots=range(SLOTS)):
            for t in slots:
                for g in range(GROUPS):
                    multiply(q, t, g)
                correct(q, t)

        def pack_run(q):
            nc.scalar.copy(
                out=r_packed[q][:].rearrange("p (f i t) -> p f t i", i=4, t=SLOTS),
                in_=r_tiles[q][:].rearrange("p t (f i) -> p f t i", i=4),
            )

        def turn_run(q):
            for j in range(TILES):
                bank = psum.tile([P, SLOTS, P], F32, name="bank", tag="bank")
                for t in range(SLOTS):
                    nc.tensor.transpose(bank[:, t, :], r_tiles[q][:, t, j * P : (j + 1) * P], ident[:])
                banks["r", q, j] = bank

        def unload(q, j, rows):
            nc.scalar.copy(out=rows[:], in_=banks["r", q, j][:].rearrange("f t m -> f m t"))

        def store(c, j, h, rows):
            f0 = c * CHUNK + j * P
            dst = out[f0 : f0 + P, GROUP * h : GROUP * (h + 1)]
            nc.sync.dma_start(out=dst, in_=rows[:].rearrange("f m t -> f (m t)"))

        def turn_upper_r2(c):
            q = STAGE_RUNS + GROUPS * c + 1
            turn_run(q)
            for j in range(TILES):
                unload(q, j, upper_rows[c, j])

        def emit_lower(c, j):
            unload(last * STAGE_RUNS + GROUPS * c, j, lower_rows[c, j])
            store(c, j, 0, lower_rows[c, j])

        def row_subtract(c, j):
            bank = psum.tile([P, GROUP], F32, name="bank", tag="bank")
            for g in range(GROUPS):
                nc.tensor.matmul_mx(
                    out=bank[:],
                    lhsT=a_codes[last, c, g][:, j * P : (j + 1) * P].bitcast(FP8X4),
                    lhsT_scale=a_scales[last, c, g][:, j * P : (j + 1) * P],
                    rhs=raw_codes[last, 1][:, g, :].bitcast(FP4X4),
                    rhs_scale=row_scales[:, g, :],
                    start=(g == 0),
                    stop=(g == GROUPS - 1),
                )
            rows = upper_rows[c, j][:].rearrange("f m t -> f (m t)")
            nc.vector.tensor_tensor(out=rows, in0=rows, in1=bank[:], op=ALU.subtract)

        def row_scale(c, j, engine):
            rows = upper_rows[c, j][:].rearrange("f m t -> f (m t)")
            engine.tensor_tensor(out=rows, in0=rows, in1=v3_row[:], op=ALU.mult)

        def emit_upper(c, j, engine):
            row_scale(c, j, engine)
            store(c, j, 1, upper_rows[c, j])

        widen_factor(0)
        for j in range(TILES):
            turn_x(0, j)
            pack_x(0, j)
        sort_codes(0, 0)
        sort_codes(0, 1)
        sort_codes(1, 0)
        quantize_x(0)
        turn_x(1, 0)
        turn_x(1, 1)
        carry_on_scalar(0, range(SLOTS))
        pack_x(1, 0)
        pack_x(1, 1)
        sort_codes(1, 1)
        carry_on_gpsimd([(1, 1)])
        steps(0, (0, 1))
        for j in (2, 3):
            turn_x(1, j)
            pack_x(1, j)
        carry_on_scalar(1, (1, 2, 3))
        sort_codes(2, 0)
        quantize_x(1)
        carry_on_gpsimd([(2, 3), (3, 3)])
        carry_on_scalar(2, (3,))
        carry_on_scalar(3, (3,))
        widen_factor(1)
        steps(0, (2, 3))
        pack_run(0)
        for q in (1, 2):
            steps(q)
            pack_run(q)
        quantize_run(0)
        quantize_run(1)

        for q in (3, 5):
            carry_on_gpsimd([(q + 1, 3), (q + 2, 2)])
            carry_on_scalar(q + 1, (3,))
            steps(q)
            pack_run(q)
            carry_on_scalar(q + 2, (2, 3))
            steps(q + 1)
            if q == STAGE_RUNS + 1:
                turn_upper_r2(0)
            else:
                widen_factor(last)
            pack_run(q + 1)
            quantize_run(q - 1)
            quantize_run(q)

        carry_on_gpsimd([(8, SLOTS), (10, SLOTS)])
        steps(7)
        pack_run(7)
        steps(8)
        for j in range(TILES - 1):
            row_subtract(0, j)
        quantize_run(6)
        quantize_run(7)
        turn_run(8)
        row_subtract(0, TILES - 1)
        for j in range(TILES):
            emit_lower(0, j)
        emit_upper(0, TILES - 1, nc.gpsimd)
        for g in range(GROUPS):
            for t in range(SLOTS - 1):
                multiply(10, t, g)
        for t in range(SLOTS - 1):
            correct(10, t)
        steps(10, (SLOTS - 1,))
        turn_upper_r2(1)
        emit_upper(0, 0, nc.gpsimd)
        emit_upper(0, 1, nc.vector)
        emit_upper(0, 2, nc.vector)
        row_subtract(1, 0)
        row_subtract(1, 1)
        turn_run(10)
        for j in (0, 1):
            emit_lower(1, j)
            emit_upper(1, j, nc.vector)
        for j in (2, 3):
            emit_lower(1, j)
        for j in (2, 3):
            row_subtract(1, j)
        for j in (2, 3):
            emit_upper(1, j, nc.vector)
